import numpy as np
import ml_dtypes


def mxq(x, axis, fmt="e4m3"):
    dtype, down = {"e4m3": (ml_dtypes.float8_e4m3fn, 7), "e5m2": (ml_dtypes.float8_e5m2, 14)}[fmt]
    v = np.moveaxis(np.asarray(x, np.float32).astype(ml_dtypes.bfloat16).astype(np.float64), axis, -1)
    blocks = v.reshape(v.shape[:-1] + (-1, 32))
    amax = np.abs(blocks).max(-1, keepdims=True)
    byte = np.maximum(np.where(amax > 0, np.frexp(amax)[1] - 1 + 127, 0) - down, 1)
    scale = np.exp2(byte - 127.0)
    codes = (blocks / scale).astype(np.float32).astype(dtype).astype(np.float64)
    return np.moveaxis((codes * scale).reshape(v.shape), -1, axis)


WIDE = False


def mx_kscale(k):
    if not WIDE:
        return np.ones(k)
    levels = np.array([10, -10, 5, -5, 0])
    if k % 512:
        return np.exp2(np.random.permutation(np.resize(levels, k // 32))).repeat(32)
    a = np.empty((k // 512, 16))
    for p in range(k // 512):
        a[p, :8] = np.random.permutation(np.resize(levels, 8))
        for g in range(8):
            far = levels[np.abs(levels - a[p, g]) >= 10]
            a[p, g + 8] = far[np.random.randint(len(far))]
    return np.exp2(a.ravel()).repeat(32)


def f64(x):
    return np.asarray(x).astype(np.float64)


def striped8(idx):
    return np.asarray(idx).reshape(8, -1, 16).transpose(0, 2, 1).reshape(128, -1).astype(np.uint16)


def unstriped8(offs):
    return offs.reshape(8, 16, -1).transpose(0, 2, 1).reshape(8, -1).astype(np.int64)


def pick8(x, idx, run):
    r = np.arange(len(x))
    return x[r[:, None], idx[r % (8 * run) // run]]


E2M1 = np.array([0.0, 0.5, 1.0, 1.5, 2.0, 3.0, 4.0, 6.0, -0.0, -0.5, -1.0, -1.5, -2.0, -3.0, -4.0, -6.0])


def pack_weight(w, fmt):
    k, n = w.shape
    w = f64(np.asarray(w, np.float32).astype(ml_dtypes.bfloat16)).reshape(k // 32, 32, n)
    amax = np.abs(w).max(1)
    if fmt == "e4m3":
        byte = np.frexp(amax)[1] - 1 + 127 - 7
    else:
        mant, ex = np.frexp(amax / 6.0)
        byte = np.where(mant > 0.5, ex, ex - 1) + 127
    byte = np.clip(np.where(amax > 0, byte, 1), 1, 254)
    scaled = (w * np.exp2(127.0 - byte)[:, None, :]).reshape(k, n).astype(np.float32)
    by_word = np.ascontiguousarray(scaled.reshape(k // 512, 128, 4, n).transpose(0, 1, 3, 2))
    if fmt == "e4m3":
        words = by_word.astype(ml_dtypes.float8_e4m3fn).view(np.uint8)
    else:
        c = by_word.astype(ml_dtypes.float4_e2m1fn).view(np.uint8) & 0xF
        words = (c[..., 0::2] | (c[..., 1::2] << 4)).reshape(k // 512, 128, 2 * n)
    return np.ascontiguousarray(words), np.ascontiguousarray(byte.astype(np.uint8).reshape(k // 512, 16, n))


def unpack_weight(words, scales, fmt):
    g, _, n = scales.shape
    words = np.ascontiguousarray(words).reshape(g, 128, n, -1)
    if fmt == "e4m3":
        vals = words.view(ml_dtypes.float8_e4m3fn).astype(np.float64)
    else:
        nib = np.empty((g, 128, n, 4), np.uint8)
        nib[..., 0::2] = words & 0xF
        nib[..., 1::2] = words >> 4
        vals = E2M1[nib]
    vals = vals * np.repeat(np.exp2(scales.astype(np.float64) - 127.0), 8, axis=1)[..., None]
    return vals.transpose(0, 1, 3, 2).reshape(g * 512, n)


D, T, U, X, I, J, Q = 512, 1024, 1024, 1024, 512, 256, 128


def setup_inputs():
    n = np.random.standard_normal
    idx = np.stack([np.random.permutation(T)[:J] for _ in range(8)])
    idx2 = np.stack([np.random.permutation(U)[:J] for _ in range(8)])
    idx3 = np.stack([np.random.permutation(X)[:I] for _ in range(8)])
    idx4 = np.stack([np.random.permutation(X)[:I] for _ in range(8)])
    idx5 = np.stack([np.random.permutation(X)[:I] for _ in range(8)])
    fd = mx_kscale(D)
    keysp = pack_weight(n((D, T)) / fd[:, None], "e2m1")
    notesp = pack_weight(n((D, U)) / fd[:, None], "e4m3")
    usersp = pack_weight(n((D, X)) / fd[:, None], "e2m1")
    return {
        "query": (n((D, Q)) * 1.0 / np.sqrt(D) * fd[:, None]).astype(np.float32),
        "keys_words": keysp[0],
        "keys_scales": keysp[1],
        "notes_words": notesp[0],
        "notes_scales": notesp[1],
        "users_words": usersp[0],
        "users_scales": usersp[1],
        "offs": striped8(idx),
        "offs2": striped8(idx2),
        "offs3": striped8(idx3),
        "offs4": striped8(idx4),
        "offs5": striped8(idx5),
    }


def reference(query, keys_words, keys_scales, notes_words, notes_scales, users_words, users_scales, offs, offs2, offs3, offs4, offs5):
    idx = unstriped8(offs)
    idx2 = unstriped8(offs2)
    idx3 = unstriped8(offs3)
    idx4 = unstriped8(offs4)
    idx5 = unstriped8(offs5)
    keysu = unpack_weight(keys_words, keys_scales, "e2m1")
    notesu = unpack_weight(notes_words, notes_scales, "e4m3")
    usersu = unpack_weight(users_words, users_scales, "e2m1")
    queryq = mxq(f64(query), 0, "e4m3")
    a = queryq.T @ keysu
    b = queryq.T @ notesu
    c0 = queryq.T @ usersu
    w = np.concatenate([pick8(a, idx, 16), pick8(b, idx2, 16)], axis=1)
    r = w - pick8(c0, idx3, 16)
    f1 = np.zeros((Q, X))
    f1[np.arange(Q)[:, None], idx4[np.arange(Q) % 128 // 16]] = r
    cc = c0 + f1
    v = pick8(cc, idx5, 16) + r
    y = np.minimum(v, w)
    return y

@@ -1,0 +1,148 @@
+from contextlib import ExitStack
+
+import concourse.mybir as mybir
+
+F32 = mybir.dt.float32
+BF16 = mybir.dt.bfloat16
+I32 = mybir.dt.int32
+U32 = mybir.dt.uint32
+U16 = mybir.dt.uint16
+U8 = mybir.dt.uint8
+FP8X4 = mybir.dt.float8_e4m3fn_x4
+FP4X4 = mybir.dt.float4_e2m1fn_x4
+ALU = mybir.AluOpType
+COPY = mybir.ActivationFunctionType.Copy
+
+P = 128
+PACK = 4
+D = 512
+Q = 128
+COLS = 1024
+SLOTS = 512
+HALF = 256
+BANK = 512
+LIST_HALF = HALF // 16
+FLOPS = 2 * D * Q * 3 * COLS
+
+
+def load_scales(queue, plane, scales):
+    for quad in range(4):
+        queue.dma_start(
+            out=plane[32 * quad : 32 * quad + 4, :].bitcast(I32),
+            in_=scales[0, 4 * quad : 4 * quad + 4, :].bitcast(I32),
+        )
+
+
+def tile_attend_halvesoff_three_kernel(
+    tc, query, keys_words, keys_scales, notes_words, notes_scales, users_words, users_scales,
+    offs, offs2, offs3, offs4, offs5, out,
+):
+    nc = tc.nc
+    with ExitStack() as ctx:
+        sb = ctx.enter_context(tc.tile_pool(name="sb", bufs=1))
+        ps = ctx.enter_context(tc.psum_pool(name="ps", bufs=1))
+
+        token_list = sb.tile([P, HALF // 16], U16, name="token_list")
+        note_list = sb.tile([P, HALF // 16], U16, name="note_list")
+        minus_list = sb.tile([P, SLOTS // 16], U16, name="minus_list")
+        put_list = sb.tile([P, SLOTS // 16], U16, name="put_list")
+        read_list = sb.tile([P, SLOTS // 16], U16, name="read_list")
+
+        users_plane = sb.tile([P, COLS], U8, name="users_plane", align_bytes=64)
+        keys_plane = sb.tile([P, COLS], U8, name="keys_plane", align_bytes=64)
+        notes_plane = sb.tile([P, COLS], U8, name="notes_plane", align_bytes=64)
+        users_codes = sb.tile([P, 2 * COLS], U8, name="users_codes", align_bytes=64)
+        keys_codes = sb.tile([P, 2 * COLS], U8, name="keys_codes", align_bytes=64)
+        notes_codes = sb.tile([P, COLS], U32, name="notes_codes", align_bytes=64)
+
+        nc.gpsimd.memset(users_plane[:].bitcast(I32), 0)
+        nc.vector.memset(keys_plane[:].bitcast(I32), 0)
+        nc.gpsimd.memset(notes_plane[:].bitcast(I32), 0)
+
+        query_raw = sb.tile([P, PACK, Q], F32, name="query_raw")
+        nc.sync.dma_start(out=query_raw[:], in_=query.rearrange("(p j) q -> p j q", j=PACK))
+        load_scales(nc.scalar, users_plane, users_scales)
+        load_scales(nc.scalar, keys_plane, keys_scales)
+        load_scales(nc.gpsimd, notes_plane, notes_scales)
+        nc.sync.dma_start(out=users_codes[:].bitcast(I32), in_=users_words[0].bitcast(I32))
+        nc.sync.dma_start(out=keys_codes[:].bitcast(I32), in_=keys_words[0].bitcast(I32))
+        nc.sync.dma_start(minus_list[:], offs3)
+        nc.sync.dma_start(
+            out=notes_codes[:].bitcast(I32),
+            in_=notes_words[0].rearrange("p n t -> p (n t)").bitcast(I32),
+        )
+        nc.sync.dma_start(token_list[:], offs)
+        nc.sync.dma_start(put_list[:], offs4)
+        nc.sync.dma_start(note_list[:], offs2)
+        nc.sync.dma_start(read_list[:], offs5)
+
+        query_bf = sb.tile([P, Q, PACK], BF16, name="query_bf", tag="reused", align_bytes=64)
+        nc.vector.tensor_copy(out=query_bf[:], in_=query_raw[:].rearrange("p j q -> p q j"))
+        query_codes = sb.tile([P, Q], U32, name="query_codes", align_bytes=64)
+        query_plane = sb.tile([P, Q], U8, name="query_plane", align_bytes=64)
+        nc.vector.quantize_mx(
+            out=query_codes[:].bitcast(FP8X4),
+            scales=query_plane[:],
+            in_=query_bf[:].rearrange("p q j -> p (q j)"),
+        )
+
+        f1 = sb.tile([P, COLS], F32, name="f1", tag="reused", align_bytes=64)
+        nc.gpsimd.memset(f1[:], 0.0)
+
+        def scores(name, codes, plane):
+            bank = ps.tile([Q, BANK], F32, name=name)
+            nc.tensor.matmul_mx(
+                out=bank[:],
+                lhsT=query_codes[:].bitcast(FP8X4),
+                lhsT_scale=query_plane[:],
+                rhs=codes,
+                rhs_scale=plane,
+                start=True,
+                stop=True,
+            )
+            return bank
+
+        def fp4_cols(codes, n):
+            return codes[:, 2 * BANK * n : 2 * BANK * (n + 1)].bitcast(FP4X4)
+
+        def cols(tile, n):
+            return tile[:, BANK * n : BANK * (n + 1)]
+
+        c0_banks = [scores("c0_bank%d" % n, fp4_cols(users_codes, n), cols(users_plane, n)) for n in range(2)]
+        a_banks = [scores("a_bank%d" % n, fp4_cols(keys_codes, n), cols(keys_plane, n)) for n in range(2)]
+        b_banks = [scores("b_bank%d" % n, cols(notes_codes, n).bitcast(FP8X4), cols(notes_plane, n)) for n in range(2)]
+
+        a = sb.tile([Q, COLS], F32, name="a")
+        b = sb.tile([Q, COLS], F32, name="b")
+        c0 = sb.tile([Q, COLS], F32, name="c0")
+        cc = sb.tile([Q, COLS], F32, name="cc")
+        w = [sb.tile([Q, HALF], F32, name="w%d" % h) for h in range(2)]
+        minus_c0 = [sb.tile([Q, HALF], F32, name="minus_c0_%d" % h) for h in range(2)]
+        gap = [sb.tile([Q, HALF], F32, name="gap%d" % h) for h in range(2)]
+        result = [sb.tile([Q, HALF], F32, name="result%d" % h) for h in range(2)]
+        cc_read = sb.tile([Q, HALF], F32, name="cc_read")
+
+        def half(offsets, h):
+            return offsets[:, LIST_HALF * h : LIST_HALF * (h + 1)]
+
+        nc.vector.tensor_copy(out=cols(c0, 0), in_=c0_banks[0][:])
+        nc.scalar.activation(cols(c0, 1), c0_banks[1][:], COPY)
+        nc.vector.tensor_scalar(minus_c0[0][:], c0[:].indirect(half(minus_list, 0)), -1.0, 0.0, ALU.mult, ALU.add)
+        nc.scalar.activation(cols(a, 0), a_banks[0][:], COPY)
+        nc.vector.tensor_copy(out=cols(a, 1), in_=a_banks[1][:])
+        nc.scalar.activation(minus_c0[1][:], c0[:].indirect(half(minus_list, 1)), COPY, scale=-1.0)
+        nc.vector.tensor_copy(out=w[0][:], in_=a[:].indirect(token_list[:]))
+        nc.vector.tensor_tensor(f1[:].indirect(half(put_list, 0)), w[0][:], minus_c0[0][:], ALU.add)
+        nc.scalar.activation(cols(b, 0), b_banks[0][:], COPY)
+        nc.scalar.activation(cols(b, 1), b_banks[1][:], COPY)
+        nc.scalar.activation(w[1][:], b[:].indirect(note_list[:]), COPY)
+        nc.vector.tensor_tensor(f1[:].indirect(half(put_list, 1)), w[1][:], minus_c0[1][:], ALU.add)
+
+        nc.vector.tensor_tensor(cc[:], c0[:], f1[:], ALU.add)
+
+        nc.vector.tensor_tensor(gap[0][:], cc[:].indirect(half(read_list, 0)), minus_c0[0][:], ALU.add)
+        nc.scalar.activation(cc_read[:], cc[:].indirect(half(read_list, 1)), COPY)
+        nc.vector.tensor_tensor(gap[1][:], cc_read[:], minus_c0[1][:], ALU.add)
+        for h, queue in ((0, nc.scalar), (1, nc.sync)):
+            nc.vector.scalar_tensor_tensor(result[h][:], gap[h][:], 0.0, w[h][:], ALU.min, ALU.add)
+            queue.dma_start(out=out[:, HALF * h : HALF * (h + 1)], in_=result[h][:])

@@ -25,8 +25,8 @@ LIST_HALF = HALF // 16
 FLOPS = 2 * D * Q * 3 * COLS
 
 
-def load_scales(queue, plane, scales):
-    for quad in range(4):
+def load_scales(queues, plane, scales):
+    for quad, queue in enumerate(queues):
         queue.dma_start(
             out=plane[32 * quad : 32 * quad + 4, :].bitcast(I32),
             in_=scales[0, 4 * quad : 4 * quad + 4, :].bitcast(I32),
@@ -56,30 +56,32 @@ def tile_attend_halvesoff_three_kernel(
         notes_codes = sb.tile([P, COLS], U32, name="notes_codes", align_bytes=64)
 
         nc.gpsimd.memset(users_plane[:].bitcast(I32), 0)
-        nc.vector.memset(keys_plane[:].bitcast(I32), 0)
+        nc.gpsimd.memset(keys_plane[:].bitcast(I32), 0)
         nc.gpsimd.memset(notes_plane[:].bitcast(I32), 0)
 
         query_raw = sb.tile([P, PACK, Q], F32, name="query_raw")
         nc.sync.dma_start(out=query_raw[:], in_=query.rearrange("(p j) q -> p j q", j=PACK))
-        load_scales(nc.scalar, users_plane, users_scales)
-        load_scales(nc.scalar, keys_plane, keys_scales)
-        load_scales(nc.gpsimd, notes_plane, notes_scales)
+        load_scales([nc.sync] * 4, users_plane, users_scales)
         nc.sync.dma_start(out=users_codes[:].bitcast(I32), in_=users_words[0].bitcast(I32))
         nc.sync.dma_start(out=keys_codes[:].bitcast(I32), in_=keys_words[0].bitcast(I32))
-        nc.sync.dma_start(minus_list[:], offs3)
+        load_scales([nc.sync] * 4, keys_plane, keys_scales)
         nc.sync.dma_start(
             out=notes_codes[:].bitcast(I32),
             in_=notes_words[0].rearrange("p n t -> p (n t)").bitcast(I32),
         )
+        nc.sync.dma_start(minus_list[:], offs3)
+        load_scales([nc.sync] * 4, notes_plane, notes_scales)
         nc.sync.dma_start(token_list[:], offs)
         nc.sync.dma_start(put_list[:], offs4)
         nc.sync.dma_start(note_list[:], offs2)
         nc.sync.dma_start(read_list[:], offs5)
 
         query_bf = sb.tile([P, Q, PACK], BF16, name="query_bf", tag="reused", align_bytes=64)
-        nc.vector.tensor_copy(out=query_bf[:], in_=query_raw[:].rearrange("p j q -> p q j"))
         query_codes = sb.tile([P, Q], U32, name="query_codes", align_bytes=64)
         query_plane = sb.tile([P, Q], U8, name="query_plane", align_bytes=64)
+        parts = [slice(0, Q // 2), slice(Q // 2, Q)]
+        nc.vector.tensor_copy(out=query_bf[:, parts[0], :], in_=query_raw[:, :, parts[0]].rearrange("p j q -> p q j"))
+        nc.scalar.activation(query_bf[:, parts[1], :], query_raw[:, :, parts[1]].rearrange("p j q -> p q j"), COPY)
         nc.vector.quantize_mx(
             out=query_codes[:].bitcast(FP8X4),
             scales=query_plane[:],
@@ -89,28 +91,19 @@ def tile_attend_halvesoff_three_kernel(
         f1 = sb.tile([P, COLS], F32, name="f1", tag="reused", align_bytes=64)
         nc.gpsimd.memset(f1[:], 0.0)
 
-        def scores(name, codes, plane):
-            bank = ps.tile([Q, BANK], F32, name=name)
+        def scores(name, codes, fmt, plane, start, width):
+            per_col = 2 if fmt == FP4X4 else 1
+            bank = ps.tile([Q, width], F32, name=name)
             nc.tensor.matmul_mx(
                 out=bank[:],
                 lhsT=query_codes[:].bitcast(FP8X4),
                 lhsT_scale=query_plane[:],
-                rhs=codes,
-                rhs_scale=plane,
+                rhs=codes[:, per_col * start : per_col * (start + width)].bitcast(fmt),
+                rhs_scale=plane[:, start : start + width],
                 start=True,
                 stop=True,
             )
             return bank
-
-        def fp4_cols(codes, n):
-            return codes[:, 2 * BANK * n : 2 * BANK * (n + 1)].bitcast(FP4X4)
-
-        def cols(tile, n):
-            return tile[:, BANK * n : BANK * (n + 1)]
-
-        c0_banks = [scores("c0_bank%d" % n, fp4_cols(users_codes, n), cols(users_plane, n)) for n in range(2)]
-        a_banks = [scores("a_bank%d" % n, fp4_cols(keys_codes, n), cols(keys_plane, n)) for n in range(2)]
-        b_banks = [scores("b_bank%d" % n, cols(notes_codes, n).bitcast(FP8X4), cols(notes_plane, n)) for n in range(2)]
 
         a = sb.tile([Q, COLS], F32, name="a")
         b = sb.tile([Q, COLS], F32, name="b")
@@ -120,29 +113,36 @@ def tile_attend_halvesoff_three_kernel(
         minus_c0 = [sb.tile([Q, HALF], F32, name="minus_c0_%d" % h) for h in range(2)]
         gap = [sb.tile([Q, HALF], F32, name="gap%d" % h) for h in range(2)]
         result = [sb.tile([Q, HALF], F32, name="result%d" % h) for h in range(2)]
-        cc_read = sb.tile([Q, HALF], F32, name="cc_read")
 
         def half(offsets, h):
             return offsets[:, LIST_HALF * h : LIST_HALF * (h + 1)]
 
-        nc.vector.tensor_copy(out=cols(c0, 0), in_=c0_banks[0][:])
-        nc.scalar.activation(cols(c0, 1), c0_banks[1][:], COPY)
+        bank = scores("c0_bank0", users_codes, FP4X4, users_plane, 0, 512)
+        nc.vector.tensor_copy(out=c0[:, 0:512], in_=bank[:])
+        bank = scores("c0_bank1", users_codes, FP4X4, users_plane, 512, 256)
+        nc.scalar.activation(c0[:, 512:768], bank[:], COPY)
+        bank = scores("c0_bank2", users_codes, FP4X4, users_plane, 768, 256)
+        nc.vector.tensor_copy(out=c0[:, 768:1024], in_=bank[:])
+        for n in range(4):
+            bank = scores("a_bank%d" % n, keys_codes, FP4X4, keys_plane, 256 * n, 256)
+            if n % 2 == 0:
+                nc.vector.tensor_copy(out=a[:, 256 * n : 256 * (n + 1)], in_=bank[:])
+            else:
+                nc.scalar.activation(a[:, 256 * n : 256 * (n + 1)], bank[:], COPY)
         nc.vector.tensor_scalar(minus_c0[0][:], c0[:].indirect(half(minus_list, 0)), -1.0, 0.0, ALU.mult, ALU.add)
-        nc.scalar.activation(cols(a, 0), a_banks[0][:], COPY)
-        nc.vector.tensor_copy(out=cols(a, 1), in_=a_banks[1][:])
         nc.scalar.activation(minus_c0[1][:], c0[:].indirect(half(minus_list, 1)), COPY, scale=-1.0)
         nc.vector.tensor_copy(out=w[0][:], in_=a[:].indirect(token_list[:]))
         nc.vector.tensor_tensor(f1[:].indirect(half(put_list, 0)), w[0][:], minus_c0[0][:], ALU.add)
-        nc.scalar.activation(cols(b, 0), b_banks[0][:], COPY)
-        nc.scalar.activation(cols(b, 1), b_banks[1][:], COPY)
+        for n in range(4):
+            bank = scores(("b_bank0", "c0_bank2", "a_bank0", "a_bank1")[n], notes_codes, FP8X4, notes_plane, 256 * n, 256)
+            nc.scalar.activation(b[:, 256 * n : 256 * (n + 1)], bank[:], COPY)
         nc.scalar.activation(w[1][:], b[:].indirect(note_list[:]), COPY)
         nc.vector.tensor_tensor(f1[:].indirect(half(put_list, 1)), w[1][:], minus_c0[1][:], ALU.add)
 
         nc.vector.tensor_tensor(cc[:], c0[:], f1[:], ALU.add)
 
-        nc.vector.tensor_tensor(gap[0][:], cc[:].indirect(half(read_list, 0)), minus_c0[0][:], ALU.add)
-        nc.scalar.activation(cc_read[:], cc[:].indirect(half(read_list, 1)), COPY)
-        nc.vector.tensor_tensor(gap[1][:], cc_read[:], minus_c0[1][:], ALU.add)
+        for h in range(2):
+            nc.vector.tensor_tensor(gap[h][:], cc[:].indirect(half(read_list, h)), minus_c0[h][:], ALU.add)
         for h, queue in ((0, nc.scalar), (1, nc.sync)):
             nc.vector.scalar_tensor_tensor(result[h][:], gap[h][:], 0.0, w[h][:], ALU.min, ALU.add)
             queue.dma_start(out=out[:, HALF * h : HALF * (h + 1)], in_=result[h][:])

from contextlib import ExitStack

import concourse.mybir as mybir

F32 = mybir.dt.float32
BF16 = mybir.dt.bfloat16
I32 = mybir.dt.int32
U32 = mybir.dt.uint32
U16 = mybir.dt.uint16
U8 = mybir.dt.uint8
FP8X4 = mybir.dt.float8_e4m3fn_x4
FP4X4 = mybir.dt.float4_e2m1fn_x4
ALU = mybir.AluOpType
COPY = mybir.ActivationFunctionType.Copy

P = 128
PACK = 4
D = 512
Q = 128
COLS = 1024
SLOTS = 512
HALF = 256
BANK = 512
LIST_HALF = HALF // 16
FLOPS = 2 * D * Q * 3 * COLS


def load_scales(queues, plane, scales):
    for quad, queue in enumerate(queues):
        queue.dma_start(
            out=plane[32 * quad : 32 * quad + 4, :].bitcast(I32),
            in_=scales[0, 4 * quad : 4 * quad + 4, :].bitcast(I32),
        )


def tile_attend_halvesoff_three_kernel(
    tc, query, keys_words, keys_scales, notes_words, notes_scales, users_words, users_scales,
    offs, offs2, offs3, offs4, offs5, out,
):
    nc = tc.nc
    with ExitStack() as ctx:
        sb = ctx.enter_context(tc.tile_pool(name="sb", bufs=1))
        ps = ctx.enter_context(tc.psum_pool(name="ps", bufs=1))

        token_list = sb.tile([P, HALF // 16], U16, name="token_list")
        note_list = sb.tile([P, HALF // 16], U16, name="note_list")
        minus_list = sb.tile([P, SLOTS // 16], U16, name="minus_list")
        put_list = sb.tile([P, SLOTS // 16], U16, name="put_list")
        read_list = sb.tile([P, SLOTS // 16], U16, name="read_list")

        users_plane = sb.tile([P, COLS], U8, name="users_plane", align_bytes=64)
        keys_plane = sb.tile([P, COLS], U8, name="keys_plane", align_bytes=64)
        notes_plane = sb.tile([P, COLS], U8, name="notes_plane", align_bytes=64)
        users_codes = sb.tile([P, 2 * COLS], U8, name="users_codes", align_bytes=64)
        keys_codes = sb.tile([P, 2 * COLS], U8, name="keys_codes", align_bytes=64)
        notes_codes = sb.tile([P, COLS], U32, name="notes_codes", align_bytes=64)

        nc.gpsimd.memset(users_plane[:].bitcast(I32), 0)
        nc.gpsimd.memset(keys_plane[:].bitcast(I32), 0)
        nc.gpsimd.memset(notes_plane[:].bitcast(I32), 0)

        query_raw = sb.tile([P, PACK, Q], F32, name="query_raw")
        nc.sync.dma_start(out=query_raw[:], in_=query.rearrange("(p j) q -> p j q", j=PACK))
        load_scales([nc.sync] * 4, users_plane, users_scales)
        nc.sync.dma_start(out=users_codes[:].bitcast(I32), in_=users_words[0].bitcast(I32))
        nc.sync.dma_start(out=keys_codes[:].bitcast(I32), in_=keys_words[0].bitcast(I32))
        load_scales([nc.sync] * 4, keys_plane, keys_scales)
        nc.sync.dma_start(
            out=notes_codes[:].bitcast(I32),
            in_=notes_words[0].rearrange("p n t -> p (n t)").bitcast(I32),
        )
        nc.sync.dma_start(minus_list[:], offs3)
        load_scales([nc.sync] * 4, notes_plane, notes_scales)
        nc.sync.dma_start(token_list[:], offs)
        nc.sync.dma_start(put_list[:], offs4)
        nc.sync.dma_start(note_list[:], offs2)
        nc.sync.dma_start(read_list[:], offs5)

        query_bf = sb.tile([P, Q, PACK], BF16, name="query_bf", tag="reused", align_bytes=64)
        query_codes = sb.tile([P, Q], U32, name="query_codes", align_bytes=64)
        query_plane = sb.tile([P, Q], U8, name="query_plane", align_bytes=64)
        parts = [slice(0, Q // 2), slice(Q // 2, Q)]
        nc.vector.tensor_copy(out=query_bf[:, parts[0], :], in_=query_raw[:, :, parts[0]].rearrange("p j q -> p q j"))
        nc.scalar.activation(query_bf[:, parts[1], :], query_raw[:, :, parts[1]].rearrange("p j q -> p q j"), COPY)
        nc.vector.quantize_mx(
            out=query_codes[:].bitcast(FP8X4),
            scales=query_plane[:],
            in_=query_bf[:].rearrange("p q j -> p (q j)"),
        )

        f1 = sb.tile([P, COLS], F32, name="f1", tag="reused", align_bytes=64)
        nc.gpsimd.memset(f1[:], 0.0)

        def scores(name, codes, fmt, plane, start, width):
            per_col = 2 if fmt == FP4X4 else 1
            bank = ps.tile([Q, width], F32, name=name)
            nc.tensor.matmul_mx(
                out=bank[:],
                lhsT=query_codes[:].bitcast(FP8X4),
                lhsT_scale=query_plane[:],
                rhs=codes[:, per_col * start : per_col * (start + width)].bitcast(fmt),
                rhs_scale=plane[:, start : start + width],
                start=True,
                stop=True,
            )
            return bank

        a = sb.tile([Q, COLS], F32, name="a")
        b = sb.tile([Q, COLS], F32, name="b")
        c0 = sb.tile([Q, COLS], F32, name="c0")
        cc = sb.tile([Q, COLS], F32, name="cc")
        w = [sb.tile([Q, HALF], F32, name="w%d" % h) for h in range(2)]
        minus_c0 = [sb.tile([Q, HALF], F32, name="minus_c0_%d" % h) for h in range(2)]
        gap = [sb.tile([Q, HALF], F32, name="gap%d" % h) for h in range(2)]
        result = [sb.tile([Q, HALF], F32, name="result%d" % h) for h in range(2)]

        def half(offsets, h):
            return offsets[:, LIST_HALF * h : LIST_HALF * (h + 1)]

        bank = scores("c0_bank0", users_codes, FP4X4, users_plane, 0, 512)
        nc.vector.tensor_copy(out=c0[:, 0:512], in_=bank[:])
        bank = scores("c0_bank1", users_codes, FP4X4, users_plane, 512, 256)
        nc.scalar.activation(c0[:, 512:768], bank[:], COPY)
        bank = scores("c0_bank2", users_codes, FP4X4, users_plane, 768, 256)
        nc.vector.tensor_copy(out=c0[:, 768:1024], in_=bank[:])
        for n in range(4):
            bank = scores("a_bank%d" % n, keys_codes, FP4X4, keys_plane, 256 * n, 256)
            if n % 2 == 0:
                nc.vector.tensor_copy(out=a[:, 256 * n : 256 * (n + 1)], in_=bank[:])
            else:
                nc.scalar.activation(a[:, 256 * n : 256 * (n + 1)], bank[:], COPY)
        nc.vector.tensor_scalar(minus_c0[0][:], c0[:].indirect(half(minus_list, 0)), -1.0, 0.0, ALU.mult, ALU.add)
        nc.scalar.activation(minus_c0[1][:], c0[:].indirect(half(minus_list, 1)), COPY, scale=-1.0)
        nc.vector.tensor_copy(out=w[0][:], in_=a[:].indirect(token_list[:]))
        nc.vector.tensor_tensor(f1[:].indirect(half(put_list, 0)), w[0][:], minus_c0[0][:], ALU.add)
        for n in range(4):
            bank = scores(("b_bank0", "c0_bank2", "a_bank0", "a_bank1")[n], notes_codes, FP8X4, notes_plane, 256 * n, 256)
            nc.scalar.activation(b[:, 256 * n : 256 * (n + 1)], bank[:], COPY)
        nc.scalar.activation(w[1][:], b[:].indirect(note_list[:]), COPY)
        nc.vector.tensor_tensor(f1[:].indirect(half(put_list, 1)), w[1][:], minus_c0[1][:], ALU.add)

        nc.vector.tensor_tensor(cc[:], c0[:], f1[:], ALU.add)

        for h in range(2):
            nc.vector.tensor_tensor(gap[h][:], cc[:].indirect(half(read_list, h)), minus_c0[h][:], ALU.add)
        for h, queue in ((0, nc.scalar), (1, nc.sync)):
            nc.vector.scalar_tensor_tensor(result[h][:], gap[h][:], 0.0, w[h][:], ALU.min, ALU.add)
            queue.dma_start(out=out[:, HALF * h : HALF * (h + 1)], in_=result[h][:])
